import numpy as np
import ml_dtypes


def mxq(x, axis, fmt="e4m3"):
    dtype, down = {"e4m3": (ml_dtypes.float8_e4m3fn, 7), "e5m2": (ml_dtypes.float8_e5m2, 14)}[fmt]
    v = np.moveaxis(np.asarray(x, np.float32).astype(ml_dtypes.bfloat16).astype(np.float64), axis, -1)
    blocks = v.reshape(v.shape[:-1] + (-1, 32))
    amax = np.abs(blocks).max(-1, keepdims=True)
    byte = np.maximum(np.where(amax > 0, np.frexp(amax)[1] - 1 + 127, 0) - down, 1)
    scale = np.exp2(byte - 127.0)
    codes = (blocks / scale).astype(np.float32).astype(dtype).astype(np.float64)
    return np.moveaxis((codes * scale).reshape(v.shape), -1, axis)


WIDE = False


def mx_kscale(k):
    if not WIDE:
        return np.ones(k)
    levels = np.array([10, -10, 5, -5, 0])
    if k % 512:
        return np.exp2(np.random.permutation(np.resize(levels, k // 32))).repeat(32)
    a = np.empty((k // 512, 16))
    for p in range(k // 512):
        a[p, :8] = np.random.permutation(np.resize(levels, 8))
        for g in range(8):
            far = levels[np.abs(levels - a[p, g]) >= 10]
            a[p, g + 8] = far[np.random.randint(len(far))]
    return np.exp2(a.ravel()).repeat(32)


def f64(x):
    return np.asarray(x).astype(np.float64)


def striped(idx):
    return np.tile(idx.reshape(-1, 16).T, (8, 1)).astype(np.uint16)


def unstriped(offs):
    return offs[:16].T.reshape(-1).astype(np.int64)


def relu2(v):
    return np.maximum(v, 0.0) ** 2


K, T, E, C, N = 1024, 1536, 8, 128, 256


def by_expert(wq, xq):
    return np.concatenate([wq[e].T @ xq[:, e * C:(e + 1) * C] for e in range(E)], axis=1)


def setup_inputs():
    n = np.random.standard_normal
    s = mx_kscale(K)[:, None]
    return {
        "xT": (n((K, T)) * s).astype(np.float32),
        "w": (n((E, K, N)) / np.sqrt(K) / s[None]).astype(np.float32),
        "b": (0.3 * n((N, E))).astype(np.float32),
        "gate": np.tile(np.random.uniform(0.2, 1.0, E * C), (K, 1)).astype(np.float32),
        "offs": striped(np.random.permutation(T)[:E * C]),
    }


def reference(xT, w, b, gate, offs):
    idx = unstriped(offs)
    xq = mxq(f64(gate) * f64(xT)[:, idx], 0, "e4m3")
    y = by_expert(mxq(f64(w), 1, "e4m3"), xq)
    y = relu2(y + np.repeat(f64(b), C, axis=1))
    out = np.zeros((N, T))
    out[:, idx] = y
    return out

@@ -1,0 +1,141 @@
+from contextlib import ExitStack
+
+import concourse.mybir as mybir
+
+K, T, E, C, N = 1024, 1536, 8, 128, 256
+SLOTS = E * C
+FLOPS = 2 * K * N * SLOTS
+BYTES = 4 * (K * T + E * K * N + N * E + SLOTS + N * T) + 2 * 128 * (SLOTS // 16)
+
+F32 = mybir.dt.float32
+BF16 = mybir.dt.bfloat16
+U32 = mybir.dt.uint32
+U16 = mybir.dt.uint16
+U8 = mybir.dt.uint8
+FP8X4 = mybir.dt.float8_e4m3fn_x4
+MULT = mybir.AluOpType.mult
+COPY = mybir.ActivationFunctionType.Copy
+RELU = mybir.ActivationFunctionType.Relu
+
+P = 128
+PACK = 4
+PASSES = K // (P * PACK)
+HALVES = N // P
+GROUPS = [512,256]
+SC = 256
+LOADS = [["x",0],["g",[0,512]],["g",[512,1024]],["x",1],["b",0],["w",0],["x",2],["w",1],["x",3],["w",2],["x",4],["w",3],["x",5],["w",4],["x",6],["w",5],["x",7],["w",6],["w",7],["w",8],["w",9],["w",10],["w",11],["w",12],["w",13],["w",14],["w",15]]
+VEC_CASTS = []
+
+
+def tile_moe_pre_lin_relu2_kernel(tc, xT, w, b, gate, offs, out):
+    nc = tc.nc
+    with ExitStack() as ctx:
+        keep = ctx.enter_context(tc.tile_pool(name="keep", bufs=1))
+        ring = ctx.enter_context(tc.tile_pool(name="ring", bufs=6))
+        psum = ctx.enter_context(tc.psum_pool(name="psum", bufs=1))
+
+        offsets = keep.tile([P, SLOTS // 16], U16, name="offsets")
+        gates = keep.tile([P, SLOTS], F32, name="gates")
+        bias = keep.tile([P, HALVES, E], F32, name="bias")
+        planes = [keep.tile([P, T], F32, name="plane%d" % i) for i in range(PASSES * PACK)]
+        w_raw = [keep.tile([P, PACK, N], F32, name="w_raw%d" % i) for i in range(E * PASSES)]
+        w_codes = [keep.tile([P, N], U32, name="w_codes%d" % i, align_bytes=64) for i in range(E * PASSES)]
+        w_scales = [keep.tile([P, N], U8, name="w_scales%d" % i, align_bytes=64) for i in range(E * PASSES)]
+        windows = [keep.tile([P, T], F32, name="window%d" % h) for h in range(HALVES)]
+        x_rows = xT.rearrange("(a p j) t -> a j p t", p=P, j=PACK)
+        w_rows = w.rearrange("e (a p j) n -> e a p j n", p=P, j=PACK)
+
+        nc.sync.dma_start(offsets[:], offs)
+        for kind, i in LOADS:
+            if kind == "x":
+                nc.sync.dma_start(planes[i][:], x_rows[i // PACK, i % PACK])
+            elif kind == "w":
+                nc.sync.dma_start(w_raw[i][:], w_rows[i // PASSES, i % PASSES])
+            elif kind == "g":
+                cols = slice(i[0], i[1])
+                nc.sync.dma_start(gates[:, cols], gate[0:P, cols])
+            else:
+                nc.sync.dma_start(bias[:], b.rearrange("(h p) e -> p h e", p=P))
+
+        for h in range(HALVES):
+            nc.vector.memset(windows[h][:], 0.0)
+
+        def interleave(dst, src, on_vector):
+            d = dst.rearrange("p (c i j) -> p c j i", i=4, j=PACK)
+            s = src.rearrange("p j (c i) -> p c j i", i=4)
+            if on_vector:
+                nc.vector.tensor_copy(d, s)
+            else:
+                nc.scalar.activation(d, s, COPY)
+
+        gathered = {}
+        x_codes = {}
+        x_scales = {}
+        for a in range(PASSES):
+            for s0 in range(0, SLOTS, GROUPS[a]):
+                gathered[a, s0] = keep.tile([P, PACK, GROUPS[a]], F32, name="gathered%d_%d" % (a, s0))
+                x_codes[a, s0] = keep.tile([P, GROUPS[a]], U32, name="x_codes%d_%d" % (a, s0), align_bytes=64)
+                x_scales[a, s0] = keep.tile([P, GROUPS[a]], U8, name="x_scales%d_%d" % (a, s0), align_bytes=64)
+
+        def do_plane(i):
+            a, j = divmod(i, PACK)
+            width = GROUPS[a]
+            for s0 in range(0, SLOTS, width):
+                picked = planes[i][:].indirect(offsets[:, s0 // 16 : (s0 + width) // 16])
+                nc.vector.tensor_tensor(gathered[a, s0][:, j, :], picked, gates[:, s0 : s0 + width], MULT)
+            if j == PACK - 1:
+                for s0 in range(0, SLOTS, width):
+                    xb = keep.tile([P, PACK * width], BF16, name="xb%d_%d" % (a, s0), align_bytes=64)
+                    interleave(xb[:], gathered[a, s0][:], False)
+                    nc.vector.quantize_mx(x_codes[a, s0][:].bitcast(FP8X4), x_scales[a, s0][:], xb[:])
+
+        def do_weights(i):
+            wb = ring.tile([P, PACK * N], BF16, name="wb", align_bytes=64)
+            interleave(wb[:], w_raw[i][:], i in VEC_CASTS)
+            nc.vector.quantize_mx(w_codes[i][:].bitcast(FP8X4), w_scales[i][:], wb[:])
+
+        def do_pair(q):
+            per = SC // C
+            for h in range(HALVES):
+                acc = psum.tile([P, SC], F32, name="acc%d_%d" % (q, h))
+                y = keep.tile([P, SC], F32, name="y%d_%d" % (q, h))
+                for r in range(per):
+                    e = q * per + r
+                    for a in range(PASSES):
+                        s0 = e * C // GROUPS[a] * GROUPS[a]
+                        cols = slice(e * C - s0, (e + 1) * C - s0)
+                        ncols = slice(h * P, (h + 1) * P)
+                        nc.tensor.matmul_mx(
+                            acc[:, r * C : (r + 1) * C],
+                            lhsT=w_codes[e * PASSES + a][:, ncols].bitcast(FP8X4),
+                            lhsT_scale=w_scales[e * PASSES + a][:, ncols],
+                            rhs=x_codes[a, s0][:, cols].bitcast(FP8X4),
+                            rhs_scale=x_scales[a, s0][:, cols],
+                            start=(a == 0),
+                            stop=(a == PASSES - 1),
+                        )
+                for r in range(per):
+                    e = q * per + r
+                    nc.scalar.activation(
+                        y[:, r * C : (r + 1) * C], acc[:, r * C : (r + 1) * C], RELU, bias=bias[:, h, e : e + 1]
+                    )
+                nc.vector.tensor_tensor(
+                    windows[h][:].indirect(offsets[:, q * SC // 16 : (q + 1) * SC // 16]), y[:], y[:], MULT
+                )
+
+        planes_done = 0
+        next_pair = 0
+        weights_done = 0
+        for kind, i in LOADS:
+            if kind == "x":
+                do_plane(i)
+                planes_done += 1
+            elif kind == "w":
+                do_weights(i)
+                weights_done += 1
+            while planes_done == PASSES * PACK and (next_pair + 1) * (SC // C) * PASSES <= weights_done:
+                do_pair(next_pair)
+                next_pair += 1
+
+        for h in range(HALVES):
+            nc.sync.dma_start(out[h * P : (h + 1) * P, :], windows[h][:])

@@ -21,10 +21,11 @@ P = 128
 PACK = 4
 PASSES = K // (P * PACK)
 HALVES = N // P
-GROUPS = [512,256]
+GROUPS = [256,256]
 SC = 256
-LOADS = [["x",0],["g",[0,512]],["g",[512,1024]],["x",1],["b",0],["w",0],["x",2],["w",1],["x",3],["w",2],["x",4],["w",3],["x",5],["w",4],["x",6],["w",5],["x",7],["w",6],["w",7],["w",8],["w",9],["w",10],["w",11],["w",12],["w",13],["w",14],["w",15]]
-VEC_CASTS = []
+LOADS = [["x",0],["g",[0,256]],["g",[256,1024]],["x",1],["b",0],["w",0],["x",2],["w",1],["x",3],["w",2],["x",4],["w",3],["x",5],["w",4],["w",5],["x",6],["w",6],["w",7],["x",7],["w",8],["w",9],["w",10],["w",11],["w",12],["w",13],["w",14],["w",15]]
+STEPS = [["G",0],["G",1],["G",2],["G",3],["I",0,0],["I",0,256],["I",0,512],["I",0,768],["G",4],["G",5],["G",6],["G",7],["C",0],["C",1],["C",2],["C",3],["C",4],["C",5],["C",6],["C",7],["C",8],["I",1,0,"C8"],["P",0,"C7"],["C",9],["I",1,256,"C9"],["C",10],["I",1,512,"C10"],["C",11],["I",1,768,"C11"],["P",1],["C",12],["C",13],["C",14],["C",15],["P",2,"C15"],["P",3]]
+VEC_CASTS = [11,15]
 
 
 def tile_moe_pre_lin_relu2_kernel(tc, xT, w, b, gate, offs, out):
@@ -38,7 +39,7 @@ def tile_moe_pre_lin_relu2_kernel(tc, xT, w, b, gate, offs, out):
         gates = keep.tile([P, SLOTS], F32, name="gates")
         bias = keep.tile([P, HALVES, E], F32, name="bias")
         planes = [keep.tile([P, T], F32, name="plane%d" % i) for i in range(PASSES * PACK)]
-        w_raw = [keep.tile([P, PACK, N], F32, name="w_raw%d" % i) for i in range(E * PASSES)]
+        w_raw = [keep.tile([P, PACK, N], F32, name="w_raw%d" % i, tag="C%d" % i, align_bytes=64) for i in range(E * PASSES)]
         w_codes = [keep.tile([P, N], U32, name="w_codes%d" % i, align_bytes=64) for i in range(E * PASSES)]
         w_scales = [keep.tile([P, N], U8, name="w_scales%d" % i, align_bytes=64) for i in range(E * PASSES)]
         windows = [keep.tile([P, T], F32, name="window%d" % h) for h in range(HALVES)]
@@ -83,22 +84,24 @@ def tile_moe_pre_lin_relu2_kernel(tc, xT, w, b, gate, offs, out):
             for s0 in range(0, SLOTS, width):
                 picked = planes[i][:].indirect(offsets[:, s0 // 16 : (s0 + width) // 16])
                 nc.vector.tensor_tensor(gathered[a, s0][:, j, :], picked, gates[:, s0 : s0 + width], MULT)
-            if j == PACK - 1:
-                for s0 in range(0, SLOTS, width):
-                    xb = keep.tile([P, PACK * width], BF16, name="xb%d_%d" % (a, s0), align_bytes=64)
-                    interleave(xb[:], gathered[a, s0][:], False)
-                    nc.vector.quantize_mx(x_codes[a, s0][:].bitcast(FP8X4), x_scales[a, s0][:], xb[:])
+
+        def do_tokens(a, s0, tag):
+            width = GROUPS[a]
+            xb = keep.tile([P, PACK * width], BF16, name="xb%d_%d" % (a, s0), tag=tag, align_bytes=64)
+            interleave(xb[:], gathered[a, s0][:], False)
+            nc.vector.quantize_mx(x_codes[a, s0][:].bitcast(FP8X4), x_scales[a, s0][:], xb[:])
 
         def do_weights(i):
             wb = ring.tile([P, PACK * N], BF16, name="wb", align_bytes=64)
             interleave(wb[:], w_raw[i][:], i in VEC_CASTS)
             nc.vector.quantize_mx(w_codes[i][:].bitcast(FP8X4), w_scales[i][:], wb[:])
 
-        def do_pair(q):
+        def do_pair(q, tag):
             per = SC // C
+            ys = keep.tile([P, HALVES * SC], F32, name="y%d" % q, tag=tag, align_bytes=64)
             for h in range(HALVES):
-                acc = psum.tile([P, SC], F32, name="acc%d_%d" % (q, h))
-                y = keep.tile([P, SC], F32, name="y%d_%d" % (q, h))
+                acc = psum.tile([P, SC], F32, name="acc%d_%d" % (q, h), tag="bank%d" % (2 * q + h))
+                y = ys[:, h * SC : (h + 1) * SC]
                 for r in range(per):
                     e = q * per + r
                     for a in range(PASSES):
@@ -120,22 +123,18 @@ def tile_moe_pre_lin_relu2_kernel(tc, xT, w, b, gate, offs, out):
                         y[:, r * C : (r + 1) * C], acc[:, r * C : (r + 1) * C], RELU, bias=bias[:, h, e : e + 1]
                     )
                 nc.vector.tensor_tensor(
-                    windows[h][:].indirect(offsets[:, q * SC // 16 : (q + 1) * SC // 16]), y[:], y[:], MULT
+                    windows[h][:].indirect(offsets[:, q * SC // 16 : (q + 1) * SC // 16]), y, y, MULT
                 )
 
-        planes_done = 0
-        next_pair = 0
-        weights_done = 0
-        for kind, i in LOADS:
-            if kind == "x":
-                do_plane(i)
-                planes_done += 1
-            elif kind == "w":
-                do_weights(i)
-                weights_done += 1
-            while planes_done == PASSES * PACK and (next_pair + 1) * (SC // C) * PASSES <= weights_done:
-                do_pair(next_pair)
-                next_pair += 1
+        for st in STEPS:
+            if st[0] == "G":
+                do_plane(st[1])
+            elif st[0] == "C":
+                do_weights(st[1])
+            elif st[0] == "I":
+                do_tokens(st[1], st[2], st[3] if len(st) > 3 else "xb%d_%d" % (st[1], st[2]))
+            else:
+                do_pair(st[1], st[2] if len(st) > 2 else "y%d" % st[1])
 
         for h in range(HALVES):
             nc.sync.dma_start(out[h * P : (h + 1) * P, :], windows[h][:])

@@ -23,8 +23,8 @@ PASSES = K // (P * PACK)
 HALVES = N // P
 GROUPS = [256,256]
 SC = 256
-LOADS = [["x",0],["g",[0,256]],["g",[256,1024]],["x",1],["b",0],["w",0],["x",2],["w",1],["x",3],["w",2],["x",4],["w",3],["x",5],["w",4],["w",5],["x",6],["w",6],["w",7],["x",7],["w",8],["w",9],["w",10],["w",11],["w",12],["w",13],["w",14],["w",15]]
-STEPS = [["G",0],["G",1],["G",2],["G",3],["I",0,0],["I",0,256],["I",0,512],["I",0,768],["G",4],["G",5],["G",6],["G",7],["C",0],["C",1],["C",2],["C",3],["C",4],["C",5],["C",6],["C",7],["C",8],["I",1,0,"C8"],["P",0,"C7"],["C",9],["I",1,256,"C9"],["C",10],["I",1,512,"C10"],["C",11],["I",1,768,"C11"],["P",1],["C",12],["C",13],["C",14],["C",15],["P",2,"C15"],["P",3]]
+LOADS = [["x",0],["g",[0,256]],["g",[256,1024]],["x",1],["b",0],["w",0],["x",2],["w",1],["x",3],["w",2],["x",4],["w",3],["x",5],["w",4],["x",6],["w",5],["w",6],["x",7],["w",7],["w",8],["w",9],["w",10],["w",11],["w",12],["w",13],["w",14],["w",15]]
+STEPS = [["G",0],["G",1],["G",2],["G",3],["I",0,0],["I",0,256],["I",0,512],["I",0,768],["G",4],["G",5],["G",6],["G",7],["C",0],["C",1],["C",2],["C",3],["C",4],["C",5],["C",6],["C",7],["I",1,0,"C7"],["P",0],["C",8],["I",1,256,"C8"],["C",9],["I",1,512,"C9"],["C",10],["I",1,768,"C10"],["C",11],["P",1,"C11"],["C",12],["C",13],["C",14],["C",15],["P",2,"C15"],["P",3]]
 VEC_CASTS = [11,15]
 
 
@@ -62,8 +62,8 @@ def tile_moe_pre_lin_relu2_kernel(tc, xT, w, b, gate, offs, out):
             nc.vector.memset(windows[h][:], 0.0)
 
         def interleave(dst, src, on_vector):
-            d = dst.rearrange("p (c i j) -> p c j i", i=4, j=PACK)
-            s = src.rearrange("p j (c i) -> p c j i", i=4)
+            d = dst.rearrange("p (c i j) -> p c j i", i=2, j=PACK)
+            s = src.rearrange("p j (c i) -> p c j i", i=2)
             if on_vector:
                 nc.vector.tensor_copy(d, s)
             else:

@@ -20,121 +20,148 @@ RELU = mybir.ActivationFunctionType.Relu
 P = 128
 PACK = 4
 PASSES = K // (P * PACK)
+PLANES = PASSES * PACK
+PIECES = E * PASSES
 HALVES = N // P
-GROUPS = [256,256]
-SC = 256
-LOADS = [["x",0],["g",[0,256]],["g",[256,1024]],["x",1],["b",0],["w",0],["x",2],["w",1],["x",3],["w",2],["x",4],["w",3],["x",5],["w",4],["x",6],["w",5],["w",6],["x",7],["w",7],["w",8],["w",9],["w",10],["w",11],["w",12],["w",13],["w",14],["w",15]]
-STEPS = [["G",0],["G",1],["G",2],["G",3],["I",0,0],["I",0,256],["I",0,512],["I",0,768],["G",4],["G",5],["G",6],["G",7],["C",0],["C",1],["C",2],["C",3],["C",4],["C",5],["C",6],["C",7],["I",1,0,"C7"],["P",0],["C",8],["I",1,256,"C8"],["C",9],["I",1,512,"C9"],["C",10],["I",1,768,"C10"],["C",11],["P",1,"C11"],["C",12],["C",13],["C",14],["C",15],["P",2,"C15"],["P",3]]
-VEC_CASTS = [11,15]
+PAIR_EXPERTS = 2
+PAIR_SLOTS = PAIR_EXPERTS * C
+PAIR_PIECES = PAIR_EXPERTS * PASSES
+PAIRS = E // PAIR_EXPERTS
+PER_COLUMN = 16
+RUN = 4
+ROUNDED_BUFS = 6
+
+EARLY_PIECES = 8
+VECTOR_ROUNDS = 3
+VECTOR_PIECES = range(EARLY_PIECES, EARLY_PIECES + 2 * VECTOR_ROUNDS, 2)
 
 
 def tile_moe_pre_lin_relu2_kernel(tc, xT, w, b, gate, offs, out):
     nc = tc.nc
     with ExitStack() as ctx:
         keep = ctx.enter_context(tc.tile_pool(name="keep", bufs=1))
-        ring = ctx.enter_context(tc.tile_pool(name="ring", bufs=6))
+        ring = ctx.enter_context(tc.tile_pool(name="ring", bufs=ROUNDED_BUFS))
         psum = ctx.enter_context(tc.psum_pool(name="psum", bufs=1))
 
-        offsets = keep.tile([P, SLOTS // 16], U16, name="offsets")
+        offsets = keep.tile([P, SLOTS // PER_COLUMN], U16, name="offsets")
         gates = keep.tile([P, SLOTS], F32, name="gates")
         bias = keep.tile([P, HALVES, E], F32, name="bias")
-        planes = [keep.tile([P, T], F32, name="plane%d" % i) for i in range(PASSES * PACK)]
-        w_raw = [keep.tile([P, PACK, N], F32, name="w_raw%d" % i, tag="C%d" % i, align_bytes=64) for i in range(E * PASSES)]
-        w_codes = [keep.tile([P, N], U32, name="w_codes%d" % i, align_bytes=64) for i in range(E * PASSES)]
-        w_scales = [keep.tile([P, N], U8, name="w_scales%d" % i, align_bytes=64) for i in range(E * PASSES)]
+        planes = [keep.tile([P, T], F32, name="plane%d" % i) for i in range(PLANES)]
+        w_raw = [
+            keep.tile([P, PACK, N], F32, name="w_raw%d" % i, tag="piece%d" % i, align_bytes=64)
+            for i in range(PIECES)
+        ]
+        w_codes = [keep.tile([P, N], U32, name="w_codes%d" % i, align_bytes=64) for i in range(PIECES)]
+        w_scales = [keep.tile([P, N], U8, name="w_scales%d" % i, align_bytes=64) for i in range(PIECES)]
         windows = [keep.tile([P, T], F32, name="window%d" % h) for h in range(HALVES)]
+        gathered = [keep.tile([P, PACK, SLOTS], F32, name="gathered%d" % a) for a in range(PASSES)]
+        x_codes = {}
+        x_scales = {}
+        for a in range(PASSES):
+            for q in range(PAIRS):
+                x_codes[a, q] = keep.tile([P, PAIR_SLOTS], U32, name="x_codes%d_%d" % (a, q), align_bytes=64)
+                x_scales[a, q] = keep.tile([P, PAIR_SLOTS], U8, name="x_scales%d_%d" % (a, q), align_bytes=64)
+
         x_rows = xT.rearrange("(a p j) t -> a j p t", p=P, j=PACK)
         w_rows = w.rearrange("e (a p j) n -> e a p j n", p=P, j=PACK)
 
+        def load_plane(i):
+            nc.sync.dma_start(planes[i][:], x_rows[i // PACK, i % PACK])
+
+        def load_piece(i):
+            nc.sync.dma_start(w_raw[i][:], w_rows[i // PASSES, i % PASSES])
+
+        def listed(first, last):
+            return offsets[:, first // PER_COLUMN : last // PER_COLUMN]
+
         nc.sync.dma_start(offsets[:], offs)
-        for kind, i in LOADS:
-            if kind == "x":
-                nc.sync.dma_start(planes[i][:], x_rows[i // PACK, i % PACK])
-            elif kind == "w":
-                nc.sync.dma_start(w_raw[i][:], w_rows[i // PASSES, i % PASSES])
-            elif kind == "g":
-                cols = slice(i[0], i[1])
-                nc.sync.dma_start(gates[:, cols], gate[0:P, cols])
-            else:
-                nc.sync.dma_start(bias[:], b.rearrange("(h p) e -> p h e", p=P))
+        load_plane(0)
+        nc.sync.dma_start(gates[:, 0:PAIR_SLOTS], gate[0:P, 0:PAIR_SLOTS])
+        nc.sync.dma_start(gates[:, PAIR_SLOTS:SLOTS], gate[0:P, PAIR_SLOTS:SLOTS])
+        load_plane(1)
+        nc.sync.dma_start(bias[:], b.rearrange("(h p) e -> p h e", p=P))
+        for i in range(2, PLANES - 1):
+            load_piece(i - 2)
+            load_plane(i)
+        for i in range(PLANES - 3, EARLY_PIECES):
+            load_piece(i)
+        load_plane(PLANES - 1)
+        for i in range(EARLY_PIECES, PIECES):
+            load_piece(i)
 
         for h in range(HALVES):
             nc.vector.memset(windows[h][:], 0.0)
 
-        def interleave(dst, src, on_vector):
-            d = dst.rearrange("p (c i j) -> p c j i", i=2, j=PACK)
-            s = src.rearrange("p j (c i) -> p c j i", i=2)
+        def round_and_interleave(rounded, rows, on_vector):
+            dst = rounded.rearrange("p (c i j) -> p c j i", i=RUN, j=PACK)
+            src = rows.rearrange("p j (c i) -> p c j i", i=RUN)
             if on_vector:
-                nc.vector.tensor_copy(d, s)
+                nc.vector.tensor_copy(dst, src)
             else:
-                nc.scalar.activation(d, s, COPY)
+                nc.scalar.activation(dst, src, COPY)
 
-        gathered = {}
-        x_codes = {}
-        x_scales = {}
-        for a in range(PASSES):
-            for s0 in range(0, SLOTS, GROUPS[a]):
-                gathered[a, s0] = keep.tile([P, PACK, GROUPS[a]], F32, name="gathered%d_%d" % (a, s0))
-                x_codes[a, s0] = keep.tile([P, GROUPS[a]], U32, name="x_codes%d_%d" % (a, s0), align_bytes=64)
-                x_scales[a, s0] = keep.tile([P, GROUPS[a]], U8, name="x_scales%d_%d" % (a, s0), align_bytes=64)
-
-        def do_plane(i):
+        def gather_plane(i):
             a, j = divmod(i, PACK)
-            width = GROUPS[a]
-            for s0 in range(0, SLOTS, width):
-                picked = planes[i][:].indirect(offsets[:, s0 // 16 : (s0 + width) // 16])
-                nc.vector.tensor_tensor(gathered[a, s0][:, j, :], picked, gates[:, s0 : s0 + width], MULT)
+            if i == 0:
+                cuts = [0, PAIR_SLOTS, SLOTS]
+            elif j == PACK - 1:
+                cuts = list(range(0, SLOTS + 1, PAIR_SLOTS))
+            else:
+                cuts = [0, SLOTS]
+            for first, last in zip(cuts[:-1], cuts[1:]):
+                picked = planes[i][:].indirect(listed(first, last))
+                nc.vector.tensor_tensor(gathered[a][:, j, first:last], picked, gates[:, first:last], MULT)
 
-        def do_tokens(a, s0, tag):
-            width = GROUPS[a]
-            xb = keep.tile([P, PACK * width], BF16, name="xb%d_%d" % (a, s0), tag=tag, align_bytes=64)
-            interleave(xb[:], gathered[a, s0][:], False)
-            nc.vector.quantize_mx(x_codes[a, s0][:].bitcast(FP8X4), x_scales[a, s0][:], xb[:])
+        def quantise_tokens(a, q):
+            rounded = keep.tile([P, PACK * PAIR_SLOTS], BF16, name="x_rounded%d_%d" % (a, q), align_bytes=64)
+            round_and_interleave(rounded[:], gathered[a][:, :, q * PAIR_SLOTS : (q + 1) * PAIR_SLOTS], False)
+            nc.vector.quantize_mx(x_codes[a, q][:].bitcast(FP8X4), x_scales[a, q][:], rounded[:])
 
-        def do_weights(i):
-            wb = ring.tile([P, PACK * N], BF16, name="wb", align_bytes=64)
-            interleave(wb[:], w_raw[i][:], i in VEC_CASTS)
-            nc.vector.quantize_mx(w_codes[i][:].bitcast(FP8X4), w_scales[i][:], wb[:])
+        def quantise_piece(i):
+            rounded = ring.tile([P, PACK * N], BF16, name="w_rounded", align_bytes=64)
+            round_and_interleave(rounded[:], w_raw[i][:], i in VECTOR_PIECES)
+            nc.vector.quantize_mx(w_codes[i][:].bitcast(FP8X4), w_scales[i][:], rounded[:])
 
-        def do_pair(q, tag):
-            per = SC // C
-            ys = keep.tile([P, HALVES * SC], F32, name="y%d" % q, tag=tag, align_bytes=64)
+        def multiply_and_scatter(q, tag):
+            relus = keep.tile([P, HALVES * PAIR_SLOTS], F32, name="relus%d" % q, tag=tag, align_bytes=64)
             for h in range(HALVES):
-                acc = psum.tile([P, SC], F32, name="acc%d_%d" % (q, h), tag="bank%d" % (2 * q + h))
-                y = ys[:, h * SC : (h + 1) * SC]
-                for r in range(per):
-                    e = q * per + r
+                sums = psum.tile([P, PAIR_SLOTS], F32, name="sums%d_%d" % (q, h))
+                relu = relus[:, h * PAIR_SLOTS : (h + 1) * PAIR_SLOTS]
+                n_cols = slice(h * P, (h + 1) * P)
+                for r in range(PAIR_EXPERTS):
+                    slot_cols = slice(r * C, (r + 1) * C)
                     for a in range(PASSES):
-                        s0 = e * C // GROUPS[a] * GROUPS[a]
-                        cols = slice(e * C - s0, (e + 1) * C - s0)
-                        ncols = slice(h * P, (h + 1) * P)
+                        i = (q * PAIR_EXPERTS + r) * PASSES + a
                         nc.tensor.matmul_mx(
-                            acc[:, r * C : (r + 1) * C],
-                            lhsT=w_codes[e * PASSES + a][:, ncols].bitcast(FP8X4),
-                            lhsT_scale=w_scales[e * PASSES + a][:, ncols],
-                            rhs=x_codes[a, s0][:, cols].bitcast(FP8X4),
-                            rhs_scale=x_scales[a, s0][:, cols],
+                            sums[:, slot_cols],
+                            lhsT=w_codes[i][:, n_cols].bitcast(FP8X4),
+                            lhsT_scale=w_scales[i][:, n_cols],
+                            rhs=x_codes[a, q][:, slot_cols].bitcast(FP8X4),
+                            rhs_scale=x_scales[a, q][:, slot_cols],
                             start=(a == 0),
                             stop=(a == PASSES - 1),
                         )
-                for r in range(per):
-                    e = q * per + r
-                    nc.scalar.activation(
-                        y[:, r * C : (r + 1) * C], acc[:, r * C : (r + 1) * C], RELU, bias=bias[:, h, e : e + 1]
-                    )
-                nc.vector.tensor_tensor(
-                    windows[h][:].indirect(offsets[:, q * SC // 16 : (q + 1) * SC // 16]), y, y, MULT
-                )
+                for r in range(PAIR_EXPERTS):
+                    slot_cols = slice(r * C, (r + 1) * C)
+                    e = q * PAIR_EXPERTS + r
+                    nc.scalar.activation(relu[:, slot_cols], sums[:, slot_cols], RELU, bias=bias[:, h, e : e + 1])
+                places = windows[h][:].indirect(listed(q * PAIR_SLOTS, (q + 1) * PAIR_SLOTS))
+                nc.vector.tensor_tensor(places, relu, relu, MULT)
 
-        for st in STEPS:
-            if st[0] == "G":
-                do_plane(st[1])
-            elif st[0] == "C":
-                do_weights(st[1])
-            elif st[0] == "I":
-                do_tokens(st[1], st[2], st[3] if len(st) > 3 else "xb%d_%d" % (st[1], st[2]))
-            else:
-                do_pair(st[1], st[2] if len(st) > 2 else "y%d" % st[1])
+        for i in range(PACK):
+            gather_plane(i)
+        for q in range(PAIRS):
+            quantise_tokens(0, q)
+        for i in range(PACK, PLANES):
+            gather_plane(i)
+
+        for q in range(PAIRS):
+            for i in range(q * PAIR_PIECES, (q + 1) * PAIR_PIECES):
+                quantise_piece(i)
+            quantise_tokens(1, q)
+            if q > 0:
+                multiply_and_scatter(q - 1, "piece%d" % ((q + 1) * PAIR_PIECES - 1))
+        multiply_and_scatter(PAIRS - 1, "last_relus")
 
         for h in range(HALVES):
             nc.sync.dma_start(out[h * P : (h + 1) * P, :], windows[h][:])

@@ -92,13 +92,10 @@ def tile_moe_pre_lin_relu2_kernel(tc, xT, w, b, gate, offs, out):
         for h in range(HALVES):
             nc.vector.memset(windows[h][:], 0.0)
 
-        def round_and_interleave(rounded, rows, on_vector):
+        def round_and_interleave(rounded, rows, move):
             dst = rounded.rearrange("p (c i j) -> p c j i", i=RUN, j=PACK)
             src = rows.rearrange("p j (c i) -> p c j i", i=RUN)
-            if on_vector:
-                nc.vector.tensor_copy(dst, src)
-            else:
-                nc.scalar.activation(dst, src, COPY)
+            move(dst, src)
 
         def gather_plane(i):
             a, j = divmod(i, PACK)
@@ -114,12 +111,18 @@ def tile_moe_pre_lin_relu2_kernel(tc, xT, w, b, gate, offs, out):
 
         def quantise_tokens(a, q):
             rounded = keep.tile([P, PACK * PAIR_SLOTS], BF16, name="x_rounded%d_%d" % (a, q), align_bytes=64)
-            round_and_interleave(rounded[:], gathered[a][:, :, q * PAIR_SLOTS : (q + 1) * PAIR_SLOTS], False)
+            round_and_interleave(rounded[:], gathered[a][:, :, q * PAIR_SLOTS : (q + 1) * PAIR_SLOTS], nc.scalar.copy)
             nc.vector.quantize_mx(x_codes[a, q][:].bitcast(FP8X4), x_scales[a, q][:], rounded[:])
 
         def quantise_piece(i):
             rounded = ring.tile([P, PACK * N], BF16, name="w_rounded", align_bytes=64)
-            round_and_interleave(rounded[:], w_raw[i][:], i in VECTOR_PIECES)
+            if i in VECTOR_PIECES:
+                move = nc.vector.tensor_copy
+            elif i == 0:
+                move = lambda dst, src: nc.scalar.activation(dst, src, COPY)
+            else:
+                move = nc.scalar.copy
+            round_and_interleave(rounded[:], w_raw[i][:], move)
             nc.vector.quantize_mx(w_codes[i][:].bitcast(FP8X4), w_scales[i][:], rounded[:])
 
         def multiply_and_scatter(q, tag):

from contextlib import ExitStack

import concourse.mybir as mybir

K, T, E, C, N = 1024, 1536, 8, 128, 256
SLOTS = E * C
FLOPS = 2 * K * N * SLOTS
BYTES = 4 * (K * T + E * K * N + N * E + SLOTS + N * T) + 2 * 128 * (SLOTS // 16)

F32 = mybir.dt.float32
BF16 = mybir.dt.bfloat16
U32 = mybir.dt.uint32
U16 = mybir.dt.uint16
U8 = mybir.dt.uint8
FP8X4 = mybir.dt.float8_e4m3fn_x4
MULT = mybir.AluOpType.mult
COPY = mybir.ActivationFunctionType.Copy
RELU = mybir.ActivationFunctionType.Relu

P = 128
PACK = 4
PASSES = K // (P * PACK)
PLANES = PASSES * PACK
PIECES = E * PASSES
HALVES = N // P
PAIR_EXPERTS = 2
PAIR_SLOTS = PAIR_EXPERTS * C
PAIR_PIECES = PAIR_EXPERTS * PASSES
PAIRS = E // PAIR_EXPERTS
PER_COLUMN = 16
RUN = 4
ROUNDED_BUFS = 6

EARLY_PIECES = 8
VECTOR_ROUNDS = 3
VECTOR_PIECES = range(EARLY_PIECES, EARLY_PIECES + 2 * VECTOR_ROUNDS, 2)


def tile_moe_pre_lin_relu2_kernel(tc, xT, w, b, gate, offs, out):
    nc = tc.nc
    with ExitStack() as ctx:
        keep = ctx.enter_context(tc.tile_pool(name="keep", bufs=1))
        ring = ctx.enter_context(tc.tile_pool(name="ring", bufs=ROUNDED_BUFS))
        psum = ctx.enter_context(tc.psum_pool(name="psum", bufs=1))

        offsets = keep.tile([P, SLOTS // PER_COLUMN], U16, name="offsets")
        gates = keep.tile([P, SLOTS], F32, name="gates")
        bias = keep.tile([P, HALVES, E], F32, name="bias")
        planes = [keep.tile([P, T], F32, name="plane%d" % i) for i in range(PLANES)]
        w_raw = [
            keep.tile([P, PACK, N], F32, name="w_raw%d" % i, tag="piece%d" % i, align_bytes=64)
            for i in range(PIECES)
        ]
        w_codes = [keep.tile([P, N], U32, name="w_codes%d" % i, align_bytes=64) for i in range(PIECES)]
        w_scales = [keep.tile([P, N], U8, name="w_scales%d" % i, align_bytes=64) for i in range(PIECES)]
        windows = [keep.tile([P, T], F32, name="window%d" % h) for h in range(HALVES)]
        gathered = [keep.tile([P, PACK, SLOTS], F32, name="gathered%d" % a) for a in range(PASSES)]
        x_codes = {}
        x_scales = {}
        for a in range(PASSES):
            for q in range(PAIRS):
                x_codes[a, q] = keep.tile([P, PAIR_SLOTS], U32, name="x_codes%d_%d" % (a, q), align_bytes=64)
                x_scales[a, q] = keep.tile([P, PAIR_SLOTS], U8, name="x_scales%d_%d" % (a, q), align_bytes=64)

        x_rows = xT.rearrange("(a p j) t -> a j p t", p=P, j=PACK)
        w_rows = w.rearrange("e (a p j) n -> e a p j n", p=P, j=PACK)

        def load_plane(i):
            nc.sync.dma_start(planes[i][:], x_rows[i // PACK, i % PACK])

        def load_piece(i):
            nc.sync.dma_start(w_raw[i][:], w_rows[i // PASSES, i % PASSES])

        def listed(first, last):
            return offsets[:, first // PER_COLUMN : last // PER_COLUMN]

        nc.sync.dma_start(offsets[:], offs)
        load_plane(0)
        nc.sync.dma_start(gates[:, 0:PAIR_SLOTS], gate[0:P, 0:PAIR_SLOTS])
        nc.sync.dma_start(gates[:, PAIR_SLOTS:SLOTS], gate[0:P, PAIR_SLOTS:SLOTS])
        load_plane(1)
        nc.sync.dma_start(bias[:], b.rearrange("(h p) e -> p h e", p=P))
        for i in range(2, PLANES - 1):
            load_piece(i - 2)
            load_plane(i)
        for i in range(PLANES - 3, EARLY_PIECES):
            load_piece(i)
        load_plane(PLANES - 1)
        for i in range(EARLY_PIECES, PIECES):
            load_piece(i)

        for h in range(HALVES):
            nc.vector.memset(windows[h][:], 0.0)

        def round_and_interleave(rounded, rows, move):
            dst = rounded.rearrange("p (c i j) -> p c j i", i=RUN, j=PACK)
            src = rows.rearrange("p j (c i) -> p c j i", i=RUN)
            move(dst, src)

        def gather_plane(i):
            a, j = divmod(i, PACK)
            if i == 0:
                cuts = [0, PAIR_SLOTS, SLOTS]
            elif j == PACK - 1:
                cuts = list(range(0, SLOTS + 1, PAIR_SLOTS))
            else:
                cuts = [0, SLOTS]
            for first, last in zip(cuts[:-1], cuts[1:]):
                picked = planes[i][:].indirect(listed(first, last))
                nc.vector.tensor_tensor(gathered[a][:, j, first:last], picked, gates[:, first:last], MULT)

        def quantise_tokens(a, q):
            rounded = keep.tile([P, PACK * PAIR_SLOTS], BF16, name="x_rounded%d_%d" % (a, q), align_bytes=64)
            round_and_interleave(rounded[:], gathered[a][:, :, q * PAIR_SLOTS : (q + 1) * PAIR_SLOTS], nc.scalar.copy)
            nc.vector.quantize_mx(x_codes[a, q][:].bitcast(FP8X4), x_scales[a, q][:], rounded[:])

        def quantise_piece(i):
            rounded = ring.tile([P, PACK * N], BF16, name="w_rounded", align_bytes=64)
            if i in VECTOR_PIECES:
                move = nc.vector.tensor_copy
            elif i == 0:
                move = lambda dst, src: nc.scalar.activation(dst, src, COPY)
            else:
                move = nc.scalar.copy
            round_and_interleave(rounded[:], w_raw[i][:], move)
            nc.vector.quantize_mx(w_codes[i][:].bitcast(FP8X4), w_scales[i][:], rounded[:])

        def multiply_and_scatter(q, tag):
            relus = keep.tile([P, HALVES * PAIR_SLOTS], F32, name="relus%d" % q, tag=tag, align_bytes=64)
            for h in range(HALVES):
                sums = psum.tile([P, PAIR_SLOTS], F32, name="sums%d_%d" % (q, h))
                relu = relus[:, h * PAIR_SLOTS : (h + 1) * PAIR_SLOTS]
                n_cols = slice(h * P, (h + 1) * P)
                for r in range(PAIR_EXPERTS):
                    slot_cols = slice(r * C, (r + 1) * C)
                    for a in range(PASSES):
                        i = (q * PAIR_EXPERTS + r) * PASSES + a
                        nc.tensor.matmul_mx(
                            sums[:, slot_cols],
                            lhsT=w_codes[i][:, n_cols].bitcast(FP8X4),
                            lhsT_scale=w_scales[i][:, n_cols],
                            rhs=x_codes[a, q][:, slot_cols].bitcast(FP8X4),
                            rhs_scale=x_scales[a, q][:, slot_cols],
                            start=(a == 0),
                            stop=(a == PASSES - 1),
                        )
                for r in range(PAIR_EXPERTS):
                    slot_cols = slice(r * C, (r + 1) * C)
                    e = q * PAIR_EXPERTS + r
                    nc.scalar.activation(relu[:, slot_cols], sums[:, slot_cols], RELU, bias=bias[:, h, e : e + 1])
                places = windows[h][:].indirect(listed(q * PAIR_SLOTS, (q + 1) * PAIR_SLOTS))
                nc.vector.tensor_tensor(places, relu, relu, MULT)

        for i in range(PACK):
            gather_plane(i)
        for q in range(PAIRS):
            quantise_tokens(0, q)
        for i in range(PACK, PLANES):
            gather_plane(i)

        for q in range(PAIRS):
            for i in range(q * PAIR_PIECES, (q + 1) * PAIR_PIECES):
                quantise_piece(i)
            quantise_tokens(1, q)
            if q > 0:
                multiply_and_scatter(q - 1, "piece%d" % ((q + 1) * PAIR_PIECES - 1))
        multiply_and_scatter(PAIRS - 1, "last_relus")

        for h in range(HALVES):
            nc.sync.dma_start(out[h * P : (h + 1) * P, :], windows[h][:])
